import numpy as np
import ml_dtypes


def mxq(x, axis, fmt="e4m3"):
    dtype, down = {"e4m3": (ml_dtypes.float8_e4m3fn, 7), "e5m2": (ml_dtypes.float8_e5m2, 14)}[fmt]
    v = np.moveaxis(np.asarray(x, np.float32).astype(ml_dtypes.bfloat16).astype(np.float64), axis, -1)
    blocks = v.reshape(v.shape[:-1] + (-1, 32))
    amax = np.abs(blocks).max(-1, keepdims=True)
    byte = np.maximum(np.where(amax > 0, np.frexp(amax)[1] - 1 + 127, 0) - down, 1)
    scale = np.exp2(byte - 127.0)
    codes = (blocks / scale).astype(np.float32).astype(dtype).astype(np.float64)
    return np.moveaxis((codes * scale).reshape(v.shape), -1, axis)


WIDE = False


def mx_kscale(k):
    if not WIDE:
        return np.ones(k)
    levels = np.array([10, -10, 5, -5, 0])
    if k % 512:
        return np.exp2(np.random.permutation(np.resize(levels, k // 32))).repeat(32)
    a = np.empty((k // 512, 16))
    for p in range(k // 512):
        a[p, :8] = np.random.permutation(np.resize(levels, 8))
        for g in range(8):
            far = levels[np.abs(levels - a[p, g]) >= 10]
            a[p, g + 8] = far[np.random.randint(len(far))]
    return np.exp2(a.ravel()).repeat(32)


BF16 = ml_dtypes.bfloat16


def bf(x):
    return np.asarray(x, np.float32).astype(BF16)


def f64(x):
    return np.asarray(x).astype(np.float64)


E2M1 = np.array([0.0, 0.5, 1.0, 1.5, 2.0, 3.0, 4.0, 6.0, -0.0, -0.5, -1.0, -1.5, -2.0, -3.0, -4.0, -6.0])


def pack_weight(w, fmt):
    k, n = w.shape
    w = f64(bf(w)).reshape(k // 32, 32, n)
    amax = np.abs(w).max(1)
    if fmt == "e4m3":
        byte = np.frexp(amax)[1] - 1 + 127 - 7
    else:
        mant, ex = np.frexp(amax / 6.0)
        byte = np.where(mant > 0.5, ex, ex - 1) + 127
    byte = np.clip(np.where(amax > 0, byte, 1), 1, 254)
    scaled = (w * np.exp2(127.0 - byte)[:, None, :]).reshape(k, n).astype(np.float32)
    by_word = np.ascontiguousarray(scaled.reshape(k // 512, 128, 4, n).transpose(0, 1, 3, 2))
    if fmt == "e4m3":
        words = by_word.astype(ml_dtypes.float8_e4m3fn).view(np.uint8)
    else:
        c = by_word.astype(ml_dtypes.float4_e2m1fn).view(np.uint8) & 0xF
        words = c[..., 0::2] | (c[..., 1::2] << 4)
    return np.ascontiguousarray(words), np.ascontiguousarray(byte.astype(np.uint8).reshape(k // 512, 16, n))


def unpack_weight(words, scales, fmt):
    g, p, n, _ = words.shape
    if fmt == "e4m3":
        vals = np.ascontiguousarray(words).view(ml_dtypes.float8_e4m3fn).astype(np.float64)
    else:
        nib = np.empty((g, p, n, 4), np.uint8)
        nib[..., 0::2] = words & 0xF
        nib[..., 1::2] = words >> 4
        vals = E2M1[nib]
    vals = vals * np.repeat(np.exp2(scales.astype(np.float64) - 127.0), 8, axis=1)[..., None]
    return vals.transpose(0, 1, 3, 2).reshape(g * 512, n)
def pack4(w):
    words, scales = pack_weight(w, "e2m1")
    return words.reshape(words.shape[0], 128, -1), scales


def unpack4(words, scales):
    return unpack_weight(words.reshape(words.shape[0], 128, -1, 2), scales, "e2m1")


def planes(Y):
    n, m = Y.shape
    b = f64(bf(Y)).reshape(n // 32, 32, m)
    amax = np.abs(b).max(1)
    byte = np.clip(np.where(amax > 0, np.frexp(amax)[1] - 1 + 127 - 7, 1), 1, 254)
    codes = (b * np.exp2(127.0 - byte)[:, None, :]).reshape(n, m).astype(np.float32).astype(ml_dtypes.float8_e4m3fn).view(np.uint8)
    words = codes.reshape(n // 512, 128, 4, m).transpose(0, 1, 3, 2)
    return np.ascontiguousarray(words), np.ascontiguousarray(byte.astype(np.uint8).reshape(n // 512, 16, m))


T, C, K, B = 1536, 512, 1024, 1024


def setup_inputs():
    s = mx_kscale(K)[:, None]
    x = bf(np.random.randn(K, T) * s)
    x_words, x_scales = pack_weight(f64(x), "e4m3")
    a = np.random.randn(C, B) / np.sqrt(K)
    b = np.random.randn(C, B) / np.sqrt(K)
    w_re = bf(np.concatenate([a, b], axis=0) / s)
    w_im = bf(np.concatenate([-b, a], axis=0) / s)
    gain = bf(0.5 * np.exp(0.6 * np.random.randn(B)))
    return {"x_words": x_words, "x_scales": x_scales,
            "w_re": w_re, "w_im": w_im, "gain": gain}


def reference(x_words, x_scales, w_re, w_im, gain):
    X = unpack_weight(x_words, x_scales, "e4m3")
    re = X.T @ mxq(f64(w_re), 0, "e4m3")
    im = X.T @ mxq(f64(w_im), 0, "e4m3")
    y = (re * re + im * im) * f64(gain)
    words, scales = planes(y.T)
    return y, words, scales

@@ -1,0 +1,288 @@
+from contextlib import ExitStack
+
+import concourse.mybir as mybir
+from concourse.masks import make_identity
+
+T, K, B = 1536, 1024, 1024
+FLOPS = 2 * 2 * T * K * B
+
+F32 = mybir.dt.float32
+BF16 = mybir.dt.bfloat16
+I32 = mybir.dt.int32
+U32 = mybir.dt.uint32
+U8 = mybir.dt.uint8
+FP8X4 = mybir.dt.float8_e4m3fn_x4
+SQUARE = mybir.ActivationFunctionType.Square
+ADD = mybir.AluOpType.add
+MULT = mybir.AluOpType.mult
+
+P = 128
+PACK = 4
+GROUP = P * PACK
+KG = K // GROUP
+HALVES = B // GROUP
+ROUND_ON_SCALAR = (4, 9, 10, 11,)
+LEAVE_ON_VECTOR = ()
+ACC_BANKS = 6
+SUMMED_ON_TENSOR = ()
+
+
+def tile_beam_power_planes_g6_kernel(tc, x_words, x_scales, w_re, w_im, gain, out_0, out_1, out_2):
+    nc = tc.nc
+    weights = (w_re, w_im)
+
+    units = [(0, t0, 2) for t0 in range(0, 12, 2)]
+    units += [(1, t0, 2) for t0 in range(0, 10, 2)] + [(1, 10, 1), (1, 11, 1)]
+    n_units = len(units)
+    pieces = [(h, m, g) for h in range(HALVES) for m in range(2) for g in range(KG)]
+
+    with ExitStack() as ctx:
+        keep = ctx.enter_context(tc.tile_pool(name="keep", bufs=1))
+        work = ctx.enter_context(tc.tile_pool(name="work", bufs=5))
+        acc_pool = ctx.enter_context(tc.psum_pool(name="acc", bufs=ACC_BANKS))
+        turn_pool = ctx.enter_context(tc.psum_pool(name="turn", bufs=8 - ACC_BANKS))
+        ctx.enter_context(tc.manual_schedule())
+
+        ident = keep.tile([P, P], F32, name="ident")
+        make_identity(nc, ident[:])
+
+        xw = keep.tile([P, KG, T], U32, name="xw", align_bytes=64)
+        xs = keep.tile([P, KG, T], U8, name="xs", align_bytes=64)
+        gain_row = keep.tile([P, B], BF16, name="gain_row")
+        raw, grouped, w_codes, w_scales = {}, {}, {}, {}
+        for pc in pieces:
+            label = "%d%d%d" % pc
+            raw[pc] = keep.tile([P, PACK, GROUP], BF16, name="raw" + label, align_bytes=64)
+            grouped[pc] = keep.tile([P, GROUP, PACK], BF16, name="grp" + label, align_bytes=64)
+            w_codes[pc] = keep.tile([P, GROUP], U32, name="wc" + label, align_bytes=64)
+            w_scales[pc] = keep.tile([P, GROUP], U8, name="ws" + label, align_bytes=64)
+        y_words = keep.tile([P, HALVES, T], U32, name="y_words", align_bytes=64)
+        y_scales = keep.tile([P, HALVES, T], U8, name="y_scales", align_bytes=64)
+        warm = keep.tile([P, 2], F32, name="warm")
+
+        nc.vector.memset(xs[:].rearrange("p g n -> p (g n)").bitcast(U32), 0)
+        nc.vector.memset(warm[:, 0:1], 0.0)
+        nc.scalar.activation(out=warm[:, 1:2], in_=warm[:, 0:1], func=SQUARE)
+
+        def load_w(i):
+            h, m, g = pieces[i]
+            rows = weights[m][g * GROUP : (g + 1) * GROUP, h * GROUP : (h + 1) * GROUP]
+            nc.sync.dma_start(out=raw[pieces[i]][:], in_=rows.rearrange("(p j) n -> p j n", j=PACK))
+
+        def load_x(t0, t1):
+            src = x_words.rearrange("g p n j -> p g (n j)")[:, :, PACK * t0 : PACK * t1]
+            nc.sync.dma_start(out=xw[:, :, t0:t1].bitcast(I32), in_=src.bitcast(I32))
+
+        def load_gain(h):
+            cols = slice(h * GROUP, (h + 1) * GROUP)
+            nc.sync.dma_start(out=gain_row[:, cols], in_=gain[cols].partition_broadcast(P))
+
+        def load_x_scales():
+            for q in range(4):
+                nc.scalar.dma_start(
+                    out=xs[32 * q : 32 * q + 4, :, :].bitcast(I32),
+                    in_=x_scales[:, 4 * q : 4 * q + 4, :].bitcast(I32).rearrange("g r n -> r g n"),
+                )
+
+        load_w(0)
+        load_w(1)
+        load_w(2)
+        load_x(0, 256)
+        load_x_scales()
+        load_w(3)
+        load_w(4)
+        load_w(5)
+        load_x(256, 768)
+        load_gain(0)
+        load_w(6)
+        load_w(7)
+        load_x(768, 1536)
+        load_gain(1)
+
+        def interleave(i, half, on_scalar):
+            cols = slice(half * 256, (half + 1) * 256)
+            dst = grouped[pieces[i]][:, cols, :].rearrange("p (c i) j -> p c j i", i=4)
+            src = raw[pieces[i]][:, :, cols].rearrange("p j (c i) -> p c j i", i=4)
+            if on_scalar:
+                nc.scalar.copy(out=dst, in_=src)
+            else:
+                nc.vector.tensor_copy(out=dst, in_=src)
+
+        def quantize_w(i):
+            pc = pieces[i]
+            nc.vector.quantize_mx(
+                out=w_codes[pc][:].bitcast(FP8X4),
+                scales=w_scales[pc][:],
+                in_=grouped[pc][:].rearrange("p n j -> p (n j)"),
+            )
+
+        summed = {}
+        acc, sq, y_f32, y_bf16, turned, y_grouped = {}, {}, {}, {}, {}, {}
+
+        def multiply(u, order):
+            h, t0, nt = units[u]
+            for i, m in order:
+                bank = acc_pool.tile([P, GROUP], F32, name="acc")
+                acc[u, i, m] = bank
+                if u in SUMMED_ON_TENSOR:
+                    beams = slice((2 * i + m) * P, (2 * i + m + 1) * P)
+                    tokens = slice(t0 * P, (t0 + 2) * P)
+                    for part in range(2):
+                        for g in range(KG):
+                            nc.tensor.matmul_mx(
+                                out=bank[:, part * 2 * P : (part + 1) * 2 * P],
+                                lhsT=w_codes[h, part, g][:, beams].bitcast(FP8X4),
+                                lhsT_scale=w_scales[h, part, g][:, beams],
+                                rhs=xw[:, g, tokens].bitcast(FP8X4),
+                                rhs_scale=xs[:, g, tokens],
+                                start=(g == 0),
+                                stop=(g == KG - 1),
+                            )
+                    continue
+                tokens = slice((t0 + i) * P, (t0 + i + 1) * P)
+                for g in range(KG):
+                    nc.tensor.matmul_mx(
+                        out=bank[:],
+                        lhsT=xw[:, g, tokens].bitcast(FP8X4),
+                        lhsT_scale=xs[:, g, tokens],
+                        rhs=w_codes[h, m, g][:].bitcast(FP8X4),
+                        rhs_scale=w_scales[h, m, g][:],
+                        start=(g == 0),
+                        stop=(g == KG - 1),
+                    )
+
+        def square(u, order):
+            for i, m in order:
+                if (u, m) not in sq:
+                    sq[u, m] = work.tile([P, 2, GROUP], F32, name="sq%d" % m)
+                nc.scalar.activation(out=sq[u, m][:, i, :], in_=acc[u, i, m][:], func=SQUARE)
+
+        def add(u):
+            nt = units[u][2]
+            nc.vector.tensor_tensor(out=sq[u, 0][:, :nt, :], in0=sq[u, 0][:, :nt, :], in1=sq[u, 1][:, :nt, :], op=ADD)
+
+        def sum_on_tensor(u):
+            for tt in range(2):
+                summed[u, tt] = turn_pool.tile([P, GROUP], F32, name="turned")
+                for bt in range(4):
+                    for part in range(2):
+                        c0 = part * 2 * P + tt * P
+                        nc.tensor.matmul(
+                            out=summed[u, tt][:, bt * P : (bt + 1) * P],
+                            lhsT=sq[u, bt % 2][:, bt // 2, c0 : c0 + P],
+                            rhs=ident[:],
+                            is_transpose=True,
+                            start=(part == 0),
+                            stop=(part == 1),
+                        )
+
+        def apply_gain(u):
+            h, t0, nt = units[u]
+            y_f32[u] = work.tile([P, 2, GROUP], F32, name="y_f32")
+            if u in SUMMED_ON_TENSOR:
+                for tt in range(2):
+                    nc.vector.tensor_tensor(
+                        out=y_f32[u][:, tt, :], in0=summed[u, tt][:], in1=gain_row[:, h * GROUP : (h + 1) * GROUP], op=MULT
+                    )
+            else:
+                row = gain_row[:, h * GROUP : (h + 1) * GROUP].unsqueeze(1).to_broadcast([P, nt, GROUP])
+                nc.vector.tensor_tensor(out=y_f32[u][:, :nt, :], in0=sq[u, 0][:, :nt, :], in1=row, op=MULT)
+            dst = out_0[t0 * P : (t0 + nt) * P, h * GROUP : (h + 1) * GROUP]
+            nc.sync.dma_start(out=dst.rearrange("(i p) b -> p i b", p=P), in_=y_f32[u][:, :nt, :])
+
+        def round_bf16(u):
+            nt = units[u][2]
+            y_bf16[u] = work.tile([P, 2, 2 * P, 2], BF16, name="y_bf16")
+            dst = y_bf16[u][:, :, : nt * P, :]
+            src = y_f32[u][:, :nt, :].rearrange("p i (m w e) -> p w (i m) e", w=2, e=2)
+            if u in ROUND_ON_SCALAR:
+                nc.scalar.copy(out=dst, in_=src)
+            else:
+                nc.vector.tensor_copy(out=dst, in_=src)
+
+        def turn(u):
+            nt = units[u][2]
+            words = y_bf16[u][:].rearrange("p w n e -> p (w n e)").bitcast(F32)
+            turned[u] = turn_pool.tile([P, 2, 2 * P], F32, name="turned")
+            for w in range(2):
+                for i in range(nt):
+                    c0 = w * 2 * P + i * P
+                    nc.tensor.transpose(turned[u][:, w, i * P : (i + 1) * P], words[:, c0 : c0 + P], ident[:])
+
+        def leave_psum(u):
+            nt = units[u][2]
+            y_grouped[u] = work.tile([P, 2 * P * PACK], BF16, name="y_grouped", align_bytes=64)
+            dst = y_grouped[u][:, : nt * P * PACK].bitcast(F32).rearrange("p (n w) -> p n w", w=2)
+            src = turned[u][:, :, : nt * P].rearrange("p w n -> p n w")
+            if u in LEAVE_ON_VECTOR:
+                nc.vector.tensor_copy(out=dst, in_=src)
+            else:
+                nc.scalar.copy(out=dst, in_=src)
+
+        def store_planes(h, c0, c1, scale_queue):
+            dst = out_1[h].rearrange("p n j -> p (n j)")[:, PACK * c0 : PACK * c1]
+            nc.sync.dma_start(out=dst.bitcast(I32), in_=y_words[:, h, c0:c1].bitcast(I32))
+
+        def store_scales(h, c0, c1, queues):
+            for q in range(4):
+                queues[q].dma_start(
+                    out=out_2[h, 4 * q : 4 * q + 4, c0:c1].bitcast(I32),
+                    in_=y_scales[32 * q : 32 * q + 4, h, c0:c1].bitcast(I32),
+                )
+
+        def quantize_y(u):
+            h, t0, nt = units[u]
+            c0, c1 = t0 * P, (t0 + nt) * P
+            nc.vector.quantize_mx(
+                out=y_words[:, h, c0:c1].bitcast(FP8X4),
+                scales=y_scales[:, h, c0:c1],
+                in_=y_grouped[u][:, : nt * P * PACK],
+            )
+            if c1 % 512 == 0:
+                store_planes(h, c1 - 512, c1, None)
+            if c1 == T:
+                store_scales(h, 0, T, [nc.sync] * 4 if h == 0 else [nc.scalar, nc.scalar, nc.sync, nc.scalar])
+
+        def tile_order(u):
+            return [(i, m) for i in range(units[u][2]) for m in range(2)]
+
+        for i in range(4):
+            interleave(i, 0, False)
+            interleave(i, 1, i in (0, 1, 2, 3,))
+            quantize_w(i)
+            if i == 1:
+                multiply(0, [(0, 0), (1, 0)])
+        multiply(0, [(0, 1), (1, 1)])
+
+        halves = [[4,0,-1,0],[4,1,-1,0],[5,0,0,1],[5,1,0,0],[6,0,1,0],[6,1,2,0],[7,0,3,0],[7,1,3,1]]
+        ready = [0,1,3,4]
+        live = lambda u: 0 <= u < n_units
+        for s in range(-1, n_units + 6):
+            order = [(0, 0), (1, 0), (0, 1), (1, 1)] if s == 0 else (tile_order(s) if live(s) else [])
+            if live(s - 3):
+                turn(s - 3)
+            for i, half, step, on_scalar in halves:
+                if step == s and on_scalar == 1:
+                    interleave(i, half, on_scalar)
+            square(s, order[:2])
+            for i, half, step, on_scalar in halves:
+                if step == s and on_scalar == 0:
+                    interleave(i, half, on_scalar)
+            if s + 1 > 0 and live(s + 1):
+                multiply(s + 1, tile_order(s + 1))
+            square(s, order[2:])
+            if live(s - 4):
+                leave_psum(s - 4)
+            if live(s - 2):
+                apply_gain(s - 2)
+            for i in range(4):
+                if ready[i] == s:
+                    quantize_w(4 + i)
+            if live(s - 1) and s - 1 not in SUMMED_ON_TENSOR:
+                add(s - 1)
+            if live(s - 2):
+                round_bf16(s - 2)
+            if s - 5 in SUMMED_ON_TENSOR:
+                sum_on_tensor(s - 5)
+            if live(s - 5):
+                quantize_y(s - 5)

@@ -21,10 +21,12 @@ PACK = 4
 GROUP = P * PACK
 KG = K // GROUP
 HALVES = B // GROUP
-ROUND_ON_SCALAR = (4, 9, 10, 11,)
+ACC_BANKS = 5
+SUMMED_ON_TENSOR = (2, 5, 8,)
+ROUND_ON_SCALAR = ()
+ROUND_ON_GPSIMD = ()
 LEAVE_ON_VECTOR = ()
-ACC_BANKS = 6
-SUMMED_ON_TENSOR = ()
+BATCHES = [[0],[1],[2],[3],[4],[5],[6],[7],[8],[9],[10],[11],[12]]
 
 
 def tile_beam_power_planes_g6_kernel(tc, x_words, x_scales, w_re, w_im, gain, out_0, out_1, out_2):
@@ -35,20 +37,28 @@ def tile_beam_power_planes_g6_kernel(tc, x_words, x_scales, w_re, w_im, gain, ou
     units += [(1, t0, 2) for t0 in range(0, 10, 2)] + [(1, 10, 1), (1, 11, 1)]
     n_units = len(units)
     pieces = [(h, m, g) for h in range(HALVES) for m in range(2) for g in range(KG)]
+    batch_of = {u: batch for batch in BATCHES for u in batch}
+
+    def batch_span(u):
+        batch = batch_of[u]
+        h, t0 = units[batch[0]][0], units[batch[0]][1]
+        return h, t0, sum(units[v][2] for v in batch)
 
     with ExitStack() as ctx:
         keep = ctx.enter_context(tc.tile_pool(name="keep", bufs=1))
-        work = ctx.enter_context(tc.tile_pool(name="work", bufs=5))
+        work = ctx.enter_context(tc.tile_pool(name="work", bufs=6))
         acc_pool = ctx.enter_context(tc.psum_pool(name="acc", bufs=ACC_BANKS))
         turn_pool = ctx.enter_context(tc.psum_pool(name="turn", bufs=8 - ACC_BANKS))
         ctx.enter_context(tc.manual_schedule())
 
+        ident_bf16 = keep.tile([P, P], BF16, name="ident_bf16")
+        make_identity(nc, ident_bf16[:])
         ident = keep.tile([P, P], F32, name="ident")
         make_identity(nc, ident[:])
 
         xw = keep.tile([P, KG, T], U32, name="xw", align_bytes=64)
         xs = keep.tile([P, KG, T], U8, name="xs", align_bytes=64)
-        gain_row = keep.tile([P, B], BF16, name="gain_row")
+        gain_cols = keep.tile([P, HALVES, PACK], BF16, name="gain_cols")
         raw, grouped, w_codes, w_scales = {}, {}, {}, {}
         for pc in pieces:
             label = "%d%d%d" % pc
@@ -58,24 +68,25 @@ def tile_beam_power_planes_g6_kernel(tc, x_words, x_scales, w_re, w_im, gain, ou
             w_scales[pc] = keep.tile([P, GROUP], U8, name="ws" + label, align_bytes=64)
         y_words = keep.tile([P, HALVES, T], U32, name="y_words", align_bytes=64)
         y_scales = keep.tile([P, HALVES, T], U8, name="y_scales", align_bytes=64)
+        y_f32 = keep.tile([P, HALVES, T // P, GROUP], F32, name="y_f32")
         warm = keep.tile([P, 2], F32, name="warm")
 
         nc.vector.memset(xs[:].rearrange("p g n -> p (g n)").bitcast(U32), 0)
         nc.vector.memset(warm[:, 0:1], 0.0)
-        nc.scalar.activation(out=warm[:, 1:2], in_=warm[:, 0:1], func=SQUARE)
 
-        def load_w(i):
+        def load_w(i, c0, c1):
             h, m, g = pieces[i]
-            rows = weights[m][g * GROUP : (g + 1) * GROUP, h * GROUP : (h + 1) * GROUP]
-            nc.sync.dma_start(out=raw[pieces[i]][:], in_=rows.rearrange("(p j) n -> p j n", j=PACK))
+            rows = weights[m][g * GROUP : (g + 1) * GROUP, h * GROUP + c0 : h * GROUP + c1]
+            nc.sync.dma_start(out=raw[pieces[i]][:, :, c0:c1], in_=rows.rearrange("(p j) n -> p j n", j=PACK))
+
+        gain_sb = keep.tile([P, HALVES, GROUP], BF16, name="gain_sb")
 
         def load_x(t0, t1):
             src = x_words.rearrange("g p n j -> p g (n j)")[:, :, PACK * t0 : PACK * t1]
             nc.sync.dma_start(out=xw[:, :, t0:t1].bitcast(I32), in_=src.bitcast(I32))
 
-        def load_gain(h):
-            cols = slice(h * GROUP, (h + 1) * GROUP)
-            nc.sync.dma_start(out=gain_row[:, cols], in_=gain[cols].partition_broadcast(P))
+        def load_gain():
+            nc.scalar.dma_start(out=gain_cols[:], in_=gain.rearrange("(h p j) -> p h j", h=HALVES, j=PACK))
 
         def load_x_scales():
             for q in range(4):
@@ -84,25 +95,26 @@ def tile_beam_power_planes_g6_kernel(tc, x_words, x_scales, w_re, w_im, gain, ou
                     in_=x_scales[:, 4 * q : 4 * q + 4, :].bitcast(I32).rearrange("g r n -> r g n"),
                 )
 
-        load_w(0)
-        load_w(1)
-        load_w(2)
-        load_x(0, 256)
-        load_x_scales()
-        load_w(3)
-        load_w(4)
-        load_w(5)
-        load_x(256, 768)
-        load_gain(0)
-        load_w(6)
-        load_w(7)
-        load_x(768, 1536)
-        load_gain(1)
 
-        def interleave(i, half, on_scalar):
-            cols = slice(half * 256, (half + 1) * 256)
-            dst = grouped[pieces[i]][:, cols, :].rearrange("p (c i) j -> p c j i", i=4)
-            src = raw[pieces[i]][:, :, cols].rearrange("p j (c i) -> p c j i", i=4)
+        spread = []
+
+        def spread_gain():
+            gain_rows = turn_pool.tile([P, HALVES, PACK, P], BF16, name="turned")
+            for h in range(HALVES):
+                for j in range(PACK):
+                    col = gain_cols[:, h, j : j + 1].to_broadcast([P, P])
+                    nc.tensor.transpose(gain_rows[:, h, j, :], col, ident_bf16[:])
+            spread.append(gain_rows)
+
+        def leave_gain():
+            gain_rows = spread[0]
+            nc.vector.tensor_copy(
+                out=gain_sb[:].rearrange("p h (m j) -> p h m j", j=PACK), in_=gain_rows[:].rearrange("p h j m -> p h m j")
+            )
+
+        def interleave(i, c0, c1, on_scalar):
+            dst = grouped[pieces[i]][:, c0:c1, :].rearrange("p (c i) j -> p c j i", i=4)
+            src = raw[pieces[i]][:, :, c0:c1].rearrange("p j (c i) -> p c j i", i=4)
             if on_scalar:
                 nc.scalar.copy(out=dst, in_=src)
             else:
@@ -116,8 +128,7 @@ def tile_beam_power_planes_g6_kernel(tc, x_words, x_scales, w_re, w_im, gain, ou
                 in_=grouped[pc][:].rearrange("p n j -> p (n j)"),
             )
 
-        summed = {}
-        acc, sq, y_f32, y_bf16, turned, y_grouped = {}, {}, {}, {}, {}, {}
+        acc, spare, summed, y_bf16, turned, y_grouped = {}, {}, {}, {}, {}, {}
 
         def multiply(u, order):
             h, t0, nt = units[u]
@@ -152,137 +163,375 @@ def tile_beam_power_planes_g6_kernel(tc, x_words, x_scales, w_re, w_im, gain, ou
                     )
 
         def square(u, order):
+            h, t0, nt = units[u]
+            last = batch_of[u][-1]
             for i, m in order:
-                if (u, m) not in sq:
-                    sq[u, m] = work.tile([P, 2, GROUP], F32, name="sq%d" % m)
-                nc.scalar.activation(out=sq[u, m][:, i, :], in_=acc[u, i, m][:], func=SQUARE)
+                if last not in spare:
+                    if u in SUMMED_ON_TENSOR:
+                        spare[last] = work.tile([P, 4, GROUP], F32, name="both", bufs=2)
+                    else:
+                        spare[last] = work.tile([P, 2, GROUP], F32, name="spare", bufs=5)
+                if u in SUMMED_ON_TENSOR:
+                    dst = spare[last][:, 2 * i + m, :]
+                elif m == 0:
+                    dst = y_f32[:, h, t0 + i, :]
+                else:
+                    dst = spare[last][:, t0 + i - batch_span(u)[1], :]
+                nc.scalar.activation(out=dst, in_=acc[u, i, m][:], func=SQUARE)
 
         def add(u):
-            nt = units[u][2]
-            nc.vector.tensor_tensor(out=sq[u, 0][:, :nt, :], in0=sq[u, 0][:, :nt, :], in1=sq[u, 1][:, :nt, :], op=ADD)
+            h, t0, nt = batch_span(u)
+            y = y_f32[:, h, t0 : t0 + nt, :]
+            nc.vector.tensor_tensor(out=y, in0=y, in1=spare[u][:, :nt, :], op=ADD)
 
-        def sum_on_tensor(u):
-            for tt in range(2):
+        def sum_on_tensor(u, tiles):
+            for tt in tiles:
                 summed[u, tt] = turn_pool.tile([P, GROUP], F32, name="turned")
                 for bt in range(4):
                     for part in range(2):
                         c0 = part * 2 * P + tt * P
                         nc.tensor.matmul(
                             out=summed[u, tt][:, bt * P : (bt + 1) * P],
-                            lhsT=sq[u, bt % 2][:, bt // 2, c0 : c0 + P],
+                            lhsT=spare[u][:, bt, c0 : c0 + P],
                             rhs=ident[:],
                             is_transpose=True,
                             start=(part == 0),
                             stop=(part == 1),
                         )
 
-        def apply_gain(u):
-            h, t0, nt = units[u]
-            y_f32[u] = work.tile([P, 2, GROUP], F32, name="y_f32")
+        def apply_gain(u, tiles):
+            h, t0, nt = batch_span(u)
+            y = y_f32[:, h, t0 : t0 + nt, :]
             if u in SUMMED_ON_TENSOR:
-                for tt in range(2):
-                    nc.vector.tensor_tensor(
-                        out=y_f32[u][:, tt, :], in0=summed[u, tt][:], in1=gain_row[:, h * GROUP : (h + 1) * GROUP], op=MULT
-                    )
+                for tt in tiles:
+                    nc.vector.tensor_tensor(out=y[:, tt, :], in0=summed[u, tt][:], in1=gain_sb[:, h, :], op=MULT)
             else:
-                row = gain_row[:, h * GROUP : (h + 1) * GROUP].unsqueeze(1).to_broadcast([P, nt, GROUP])
-                nc.vector.tensor_tensor(out=y_f32[u][:, :nt, :], in0=sq[u, 0][:, :nt, :], in1=row, op=MULT)
-            dst = out_0[t0 * P : (t0 + nt) * P, h * GROUP : (h + 1) * GROUP]
-            nc.sync.dma_start(out=dst.rearrange("(i p) b -> p i b", p=P), in_=y_f32[u][:, :nt, :])
+                row = gain_sb[:, h, :].unsqueeze(1).to_broadcast([P, nt, GROUP])
+                nc.vector.tensor_tensor(out=y, in0=y, in1=row, op=MULT)
 
-        def round_bf16(u):
-            nt = units[u][2]
-            y_bf16[u] = work.tile([P, 2, 2 * P, 2], BF16, name="y_bf16")
-            dst = y_bf16[u][:, :, : nt * P, :]
-            src = y_f32[u][:, :nt, :].rearrange("p i (m w e) -> p w (i m) e", w=2, e=2)
-            if u in ROUND_ON_SCALAR:
+        def store_y(u):
+            h, t0, nt = batch_span(u)
+            y = y_f32[:, h, t0 : t0 + nt, :]
+            dst = out_0[t0 * P : (t0 + nt) * P, h * GROUP : (h + 1) * GROUP]
+            nc.sync.dma_start(out=dst.rearrange("(i p) b -> p i b", p=P), in_=y)
+
+        def round_bf16(u, on_scalar):
+            h, t0, nt = batch_span(u)
+            y_bf16[u] = work.tile([P, 2 * GROUP], BF16, name="y_bf16")
+            y = y_f32[:, h, t0 : t0 + nt, :]
+            if nt == 1:
+                dst = y_bf16[u][:, :GROUP].rearrange("p (w a m e) -> p a w m e", a=2, w=2, e=2)
+                src = y.rearrange("p i (a m w e) -> p (i a) w m e", a=2, w=2, e=2)
+            else:
+                dst = y_bf16[u][:, : nt * GROUP].rearrange("p (i w m e) -> p i w m e", i=nt, w=2, e=2)
+                src = y.rearrange("p i (m w e) -> p i w m e", w=2, e=2)
+            if on_scalar:
                 nc.scalar.copy(out=dst, in_=src)
+            elif u in ROUND_ON_GPSIMD:
+                nc.gpsimd.tensor_scalar(out=dst, in0=src, scalar1=1.0, scalar2=0.0, op0=MULT, op1=ADD)
             else:
                 nc.vector.tensor_copy(out=dst, in_=src)
 
         def turn(u):
-            nt = units[u][2]
-            words = y_bf16[u][:].rearrange("p w n e -> p (w n e)").bitcast(F32)
+            h, t0, nt = units[u]
+            words = y_bf16[batch_of[u][-1]][:].bitcast(F32)
             turned[u] = turn_pool.tile([P, 2, 2 * P], F32, name="turned")
-            for w in range(2):
-                for i in range(nt):
-                    c0 = w * 2 * P + i * P
+            for i in range(nt):
+                for w in range(2):
+                    c0 = (2 * (t0 + i - batch_span(u)[1]) + w) * P
                     nc.tensor.transpose(turned[u][:, w, i * P : (i + 1) * P], words[:, c0 : c0 + P], ident[:])
 
-        def leave_psum(u):
-            nt = units[u][2]
-            y_grouped[u] = work.tile([P, 2 * P * PACK], BF16, name="y_grouped", align_bytes=64)
-            dst = y_grouped[u][:, : nt * P * PACK].bitcast(F32).rearrange("p (n w) -> p n w", w=2)
+        def leave_psum(u, on_scalar):
+            h, t0, nt = units[u]
+            last = batch_of[u][-1]
+            if last not in y_grouped:
+                y_grouped[last] = work.tile([P, 2 * GROUP], BF16, name="y_grouped", align_bytes=64)
+            c0 = (t0 - batch_span(u)[1]) * GROUP
+            dst = y_grouped[last][:, c0 : c0 + nt * GROUP].bitcast(F32).rearrange("p (n w) -> p n w", w=2)
             src = turned[u][:, :, : nt * P].rearrange("p w n -> p n w")
-            if u in LEAVE_ON_VECTOR:
+            if not on_scalar:
                 nc.vector.tensor_copy(out=dst, in_=src)
             else:
                 nc.scalar.copy(out=dst, in_=src)
 
-        def store_planes(h, c0, c1, scale_queue):
-            dst = out_1[h].rearrange("p n j -> p (n j)")[:, PACK * c0 : PACK * c1]
-            nc.sync.dma_start(out=dst.bitcast(I32), in_=y_words[:, h, c0:c1].bitcast(I32))
-
-        def store_scales(h, c0, c1, queues):
-            for q in range(4):
-                queues[q].dma_start(
-                    out=out_2[h, 4 * q : 4 * q + 4, c0:c1].bitcast(I32),
-                    in_=y_scales[32 * q : 32 * q + 4, h, c0:c1].bitcast(I32),
-                )
-
         def quantize_y(u):
-            h, t0, nt = units[u]
+            h, t0, nt = batch_span(u)
             c0, c1 = t0 * P, (t0 + nt) * P
             nc.vector.quantize_mx(
                 out=y_words[:, h, c0:c1].bitcast(FP8X4),
                 scales=y_scales[:, h, c0:c1],
-                in_=y_grouped[u][:, : nt * P * PACK],
+                in_=y_grouped[u][:, : nt * GROUP],
             )
-            if c1 % 512 == 0:
-                store_planes(h, c1 - 512, c1, None)
-            if c1 == T:
-                store_scales(h, 0, T, [nc.sync] * 4 if h == 0 else [nc.scalar, nc.scalar, nc.sync, nc.scalar])
+
+        def store_words(u):
+            h, t0, nt = batch_span(u)
+            c1 = (t0 + nt) * P
+            word_cuts = [0, 512, 1024, T] if h == 0 else [0, 512, 1024, T]
+            if c1 in word_cuts:
+                w0 = word_cuts[word_cuts.index(c1) - 1]
+                dst = out_1[h].rearrange("p n j -> p (n j)")[:, PACK * w0 : PACK * c1]
+                nc.sync.dma_start(out=dst.bitcast(I32), in_=y_words[:, h, w0:c1].bitcast(I32))
+
+        def store_scales(u, q):
+            h, t0, nt = batch_span(u)
+            c1 = (t0 + nt) * P
+            scale_cuts = [0, T] if h == 0 else [0, T]
+            if c1 in scale_cuts:
+                w0 = scale_cuts[scale_cuts.index(c1) - 1]
+                queues = [nc.scalar, nc.scalar, nc.sync, nc.scalar] if u == n_units - 1 else [nc.sync] * 4
+                if True:
+                    queues[q].dma_start(
+                        out=out_2[h, 4 * q : 4 * q + 4, w0:c1].bitcast(I32),
+                        in_=y_scales[32 * q : 32 * q + 4, h, w0:c1].bitcast(I32),
+                    )
 
         def tile_order(u):
             return [(i, m) for i in range(units[u][2]) for m in range(2)]
 
-        for i in range(4):
-            interleave(i, 0, False)
-            interleave(i, 1, i in (0, 1, 2, 3,))
-            quantize_w(i)
-            if i == 1:
-                multiply(0, [(0, 0), (1, 0)])
-        multiply(0, [(0, 1), (1, 1)])
-
-        halves = [[4,0,-1,0],[4,1,-1,0],[5,0,0,1],[5,1,0,0],[6,0,1,0],[6,1,2,0],[7,0,3,0],[7,1,3,1]]
-        ready = [0,1,3,4]
-        live = lambda u: 0 <= u < n_units
-        for s in range(-1, n_units + 6):
-            order = [(0, 0), (1, 0), (0, 1), (1, 1)] if s == 0 else (tile_order(s) if live(s) else [])
-            if live(s - 3):
-                turn(s - 3)
-            for i, half, step, on_scalar in halves:
-                if step == s and on_scalar == 1:
-                    interleave(i, half, on_scalar)
-            square(s, order[:2])
-            for i, half, step, on_scalar in halves:
-                if step == s and on_scalar == 0:
-                    interleave(i, half, on_scalar)
-            if s + 1 > 0 and live(s + 1):
-                multiply(s + 1, tile_order(s + 1))
-            square(s, order[2:])
-            if live(s - 4):
-                leave_psum(s - 4)
-            if live(s - 2):
-                apply_gain(s - 2)
-            for i in range(4):
-                if ready[i] == s:
-                    quantize_w(4 + i)
-            if live(s - 1) and s - 1 not in SUMMED_ON_TENSOR:
-                add(s - 1)
-            if live(s - 2):
-                round_bf16(s - 2)
-            if s - 5 in SUMMED_ON_TENSOR:
-                sum_on_tensor(s - 5)
-            if live(s - 5):
-                quantize_y(s - 5)
+        load_gain()
+        load_x_scales()
+        nc.scalar.activation(out=warm[:, 1:2], in_=warm[:, 0:1], func=SQUARE)
+        load_w(0, 0, 512)
+        interleave(0, 0, 256, True)
+        load_w(1, 0, 512)
+        interleave(0, 256, 512, False)
+        interleave(1, 0, 256, False)
+        load_w(2, 0, 512)
+        interleave(1, 256, 512, True)
+        quantize_w(0)
+        interleave(2, 0, 256, False)
+        load_w(3, 0, 512)
+        load_x(0, 256)
+        load_w(4, 0, 512)
+        interleave(2, 256, 512, True)
+        quantize_w(1)
+        spread_gain()
+        interleave(3, 0, 256, False)
+        multiply(0, [(0, 0)])
+        multiply(0, [(1, 0)])
+        quantize_w(2)
+        interleave(3, 256, 512, True)
+        quantize_w(3)
+        load_w(5, 0, 512)
+        multiply(0, [(0, 1)])
+        load_x(256, 768)
+        multiply(0, [(1, 1)])
+        interleave(4, 0, 256, True)
+        square(0, [(1, 0)])
+        square(0, [(0, 0)])
+        multiply(1, [(0, 0)])
+        multiply(1, [(0, 1)])
+        square(0, [(1, 1)])
+        square(0, [(0, 1)])
+        square(1, [(0, 1)])
+        square(1, [(0, 0)])
+        load_w(6, 0, 512)
+        multiply(1, [(1, 0)])
+        multiply(1, [(1, 1)])
+        multiply(2, [(0, 0)])
+        square(1, [(1, 1)])
+        multiply(2, [(0, 1)])
+        multiply(2, [(1, 0)])
+        leave_gain()
+        square(1, [(1, 0)])
+        load_x(768, 1536)
+        square(2, [(0, 1)])
+        multiply(2, [(1, 1)])
+        square(2, [(0, 0)])
+        load_w(7, 0, 512)
+        multiply(3, [(0, 0)])
+        multiply(3, [(0, 1)])
+        interleave(5, 0, 256, False)
+        interleave(5, 256, 512, False)
+        interleave(4, 256, 512, False)
+        interleave(6, 256, 512, False)
+        multiply(3, [(1, 0)])
+        add(0)
+        square(2, [(1, 1)])
+        quantize_w(4)
+        square(2, [(1, 0)])
+        quantize_w(5)
+        square(3, [(0, 1)])
+        square(3, [(0, 0)])
+        multiply(3, [(1, 1)])
+        square(3, [(1, 1)])
+        square(3, [(1, 0)])
+        multiply(4, [(0, 0)])
+        multiply(4, [(0, 1)])
+        multiply(4, [(1, 0)])
+        add(1)
+        multiply(4, [(1, 1)])
+        interleave(6, 0, 256, False)
+        interleave(7, 256, 512, False)
+        square(4, [(0, 1)])
+        apply_gain(0, [0])
+        store_y(0)
+        apply_gain(1, [0])
+        store_y(1)
+        quantize_w(6)
+        multiply(5, [(0, 0)])
+        interleave(7, 0, 256, False)
+        square(4, [(0, 0)])
+        square(4, [(1, 1)])
+        add(3)
+        round_bf16(0, True)
+        square(4, [(1, 0)])
+        multiply(5, [(0, 1)])
+        sum_on_tensor(2, [0])
+        quantize_w(7)
+        square(5, [(0, 1)])
+        square(5, [(0, 0)])
+        sum_on_tensor(2, [1])
+        multiply(5, [(1, 0)])
+        multiply(5, [(1, 1)])
+        apply_gain(2, [0])
+        multiply(6, [(0, 0)])
+        multiply(6, [(0, 1)])
+        multiply(6, [(1, 0)])
+        square(5, [(1, 1)])
+        apply_gain(2, [1])
+        store_y(2)
+        round_bf16(1, False)
+        round_bf16(2, False)
+        add(4)
+        square(5, [(1, 0)])
+        multiply(6, [(1, 1)])
+        multiply(7, [(0, 0)])
+        apply_gain(3, [0])
+        store_y(3)
+        apply_gain(4, [0])
+        store_y(4)
+        square(6, [(0, 1)])
+        turn(0)
+        square(6, [(0, 0)])
+        turn(1)
+        leave_psum(0, False)
+        square(6, [(1, 1)])
+        square(6, [(1, 0)])
+        multiply(7, [(0, 1)])
+        round_bf16(3, False)
+        add(6)
+        multiply(7, [(1, 0)])
+        leave_psum(1, True)
+        multiply(7, [(1, 1)])
+        quantize_y(0)
+        sum_on_tensor(5, [0])
+        square(7, [(0, 1)])
+        turn(2)
+        square(7, [(0, 0)])
+        sum_on_tensor(5, [1])
+        square(7, [(1, 1)])
+        apply_gain(5, [0])
+        square(7, [(1, 0)])
+        multiply(8, [(0, 0)])
+        multiply(8, [(0, 1)])
+        leave_psum(2, True)
+        round_bf16(4, True)
+        add(7)
+        multiply(8, [(1, 0)])
+        multiply(8, [(1, 1)])
+        apply_gain(5, [1])
+        store_y(5)
+        multiply(9, [(0, 0)])
+        square(8, [(0, 1)])
+        square(8, [(0, 0)])
+        apply_gain(6, [0])
+        store_y(6)
+        round_bf16(5, False)
+        square(8, [(1, 1)])
+        multiply(9, [(0, 1)])
+        turn(3)
+        turn(4)
+        quantize_y(1)
+        store_words(1)
+        square(8, [(1, 0)])
+        turn(5)
+        square(9, [(0, 1)])
+        leave_psum(3, True)
+        leave_psum(4, True)
+        multiply(9, [(1, 0)])
+        square(9, [(0, 0)])
+        multiply(9, [(1, 1)])
+        apply_gain(7, [0])
+        store_y(7)
+        sum_on_tensor(8, [0])
+        round_bf16(6, False)
+        sum_on_tensor(8, [1])
+        multiply(10, [(0, 0)])
+        quantize_y(2)
+        multiply(10, [(0, 1)])
+        square(9, [(1, 1)])
+        square(9, [(1, 0)])
+        quantize_y(3)
+        store_words(3)
+        round_bf16(7, True)
+        square(10, [(0, 1)])
+        multiply(10, [(1, 0)])
+        square(10, [(0, 0)])
+        leave_psum(5, False)
+        quantize_y(4)
+        apply_gain(8, [0])
+        multiply(10, [(1, 1)])
+        multiply(11, [(0, 0)])
+        quantize_y(5)
+        store_words(5)
+        store_scales(5, 0)
+        store_scales(5, 1)
+        store_scales(5, 2)
+        store_scales(5, 3)
+        square(10, [(1, 1)])
+        square(10, [(1, 0)])
+        add(9)
+        apply_gain(8, [1])
+        store_y(8)
+        apply_gain(9, [0])
+        store_y(9)
+        multiply(11, [(0, 1)])
+        square(11, [(0, 1)])
+        round_bf16(8, False)
+        multiply(12, [(0, 0)])
+        round_bf16(9, False)
+        multiply(12, [(0, 1)])
+        square(11, [(0, 0)])
+        turn(6)
+        square(12, [(0, 1)])
+        square(12, [(0, 0)])
+        add(10)
+        add(11)
+        leave_psum(6, True)
+        apply_gain(10, [0])
+        store_y(10)
+        turn(7)
+        add(12)
+        turn(8)
+        leave_psum(7, True)
+        apply_gain(11, [0])
+        store_y(11)
+        apply_gain(12, [0])
+        store_y(12)
+        round_bf16(10, True)
+        round_bf16(11, False)
+        leave_psum(8, True)
+        quantize_y(6)
+        turn(9)
+        turn(10)
+        round_bf16(12, False)
+        quantize_y(7)
+        store_words(7)
+        quantize_y(8)
+        leave_psum(9, True)
+        leave_psum(10, True)
+        turn(11)
+        quantize_y(9)
+        store_words(9)
+        turn(12)
+        leave_psum(11, True)
+        quantize_y(10)
+        leave_psum(12, True)
+        quantize_y(11)
+        quantize_y(12)
+        store_words(12)
+        store_scales(12, 0)
+        store_scales(12, 1)
+        store_scales(12, 2)
+        store_scales(12, 3)

from contextlib import ExitStack

import concourse.mybir as mybir
from concourse.masks import make_identity

T, K, B = 1536, 1024, 1024
FLOPS = 2 * 2 * T * K * B

F32 = mybir.dt.float32
BF16 = mybir.dt.bfloat16
I32 = mybir.dt.int32
U32 = mybir.dt.uint32
U8 = mybir.dt.uint8
FP8X4 = mybir.dt.float8_e4m3fn_x4
SQUARE = mybir.ActivationFunctionType.Square
ADD = mybir.AluOpType.add
MULT = mybir.AluOpType.mult

P = 128
PACK = 4
GROUP = P * PACK
KG = K // GROUP
HALVES = B // GROUP
ACC_BANKS = 5
SUMMED_ON_TENSOR = (2, 5, 8,)
ROUND_ON_SCALAR = ()
ROUND_ON_GPSIMD = ()
LEAVE_ON_VECTOR = ()
BATCHES = [[0],[1],[2],[3],[4],[5],[6],[7],[8],[9],[10],[11],[12]]


def tile_beam_power_planes_g6_kernel(tc, x_words, x_scales, w_re, w_im, gain, out_0, out_1, out_2):
    nc = tc.nc
    weights = (w_re, w_im)

    units = [(0, t0, 2) for t0 in range(0, 12, 2)]
    units += [(1, t0, 2) for t0 in range(0, 10, 2)] + [(1, 10, 1), (1, 11, 1)]
    n_units = len(units)
    pieces = [(h, m, g) for h in range(HALVES) for m in range(2) for g in range(KG)]
    batch_of = {u: batch for batch in BATCHES for u in batch}

    def batch_span(u):
        batch = batch_of[u]
        h, t0 = units[batch[0]][0], units[batch[0]][1]
        return h, t0, sum(units[v][2] for v in batch)

    with ExitStack() as ctx:
        keep = ctx.enter_context(tc.tile_pool(name="keep", bufs=1))
        work = ctx.enter_context(tc.tile_pool(name="work", bufs=6))
        acc_pool = ctx.enter_context(tc.psum_pool(name="acc", bufs=ACC_BANKS))
        turn_pool = ctx.enter_context(tc.psum_pool(name="turn", bufs=8 - ACC_BANKS))
        ctx.enter_context(tc.manual_schedule())

        ident_bf16 = keep.tile([P, P], BF16, name="ident_bf16")
        make_identity(nc, ident_bf16[:])
        ident = keep.tile([P, P], F32, name="ident")
        make_identity(nc, ident[:])

        xw = keep.tile([P, KG, T], U32, name="xw", align_bytes=64)
        xs = keep.tile([P, KG, T], U8, name="xs", align_bytes=64)
        gain_cols = keep.tile([P, HALVES, PACK], BF16, name="gain_cols")
        raw, grouped, w_codes, w_scales = {}, {}, {}, {}
        for pc in pieces:
            label = "%d%d%d" % pc
            raw[pc] = keep.tile([P, PACK, GROUP], BF16, name="raw" + label, align_bytes=64)
            grouped[pc] = keep.tile([P, GROUP, PACK], BF16, name="grp" + label, align_bytes=64)
            w_codes[pc] = keep.tile([P, GROUP], U32, name="wc" + label, align_bytes=64)
            w_scales[pc] = keep.tile([P, GROUP], U8, name="ws" + label, align_bytes=64)
        y_words = keep.tile([P, HALVES, T], U32, name="y_words", align_bytes=64)
        y_scales = keep.tile([P, HALVES, T], U8, name="y_scales", align_bytes=64)
        y_f32 = keep.tile([P, HALVES, T // P, GROUP], F32, name="y_f32")
        warm = keep.tile([P, 2], F32, name="warm")

        nc.vector.memset(xs[:].rearrange("p g n -> p (g n)").bitcast(U32), 0)
        nc.vector.memset(warm[:, 0:1], 0.0)

        def load_w(i, c0, c1):
            h, m, g = pieces[i]
            rows = weights[m][g * GROUP : (g + 1) * GROUP, h * GROUP + c0 : h * GROUP + c1]
            nc.sync.dma_start(out=raw[pieces[i]][:, :, c0:c1], in_=rows.rearrange("(p j) n -> p j n", j=PACK))

        gain_sb = keep.tile([P, HALVES, GROUP], BF16, name="gain_sb")

        def load_x(t0, t1):
            src = x_words.rearrange("g p n j -> p g (n j)")[:, :, PACK * t0 : PACK * t1]
            nc.sync.dma_start(out=xw[:, :, t0:t1].bitcast(I32), in_=src.bitcast(I32))

        def load_gain():
            nc.scalar.dma_start(out=gain_cols[:], in_=gain.rearrange("(h p j) -> p h j", h=HALVES, j=PACK))

        def load_x_scales():
            for q in range(4):
                nc.scalar.dma_start(
                    out=xs[32 * q : 32 * q + 4, :, :].bitcast(I32),
                    in_=x_scales[:, 4 * q : 4 * q + 4, :].bitcast(I32).rearrange("g r n -> r g n"),
                )


        spread = []

        def spread_gain():
            gain_rows = turn_pool.tile([P, HALVES, PACK, P], BF16, name="turned")
            for h in range(HALVES):
                for j in range(PACK):
                    col = gain_cols[:, h, j : j + 1].to_broadcast([P, P])
                    nc.tensor.transpose(gain_rows[:, h, j, :], col, ident_bf16[:])
            spread.append(gain_rows)

        def leave_gain():
            gain_rows = spread[0]
            nc.vector.tensor_copy(
                out=gain_sb[:].rearrange("p h (m j) -> p h m j", j=PACK), in_=gain_rows[:].rearrange("p h j m -> p h m j")
            )

        def interleave(i, c0, c1, on_scalar):
            dst = grouped[pieces[i]][:, c0:c1, :].rearrange("p (c i) j -> p c j i", i=4)
            src = raw[pieces[i]][:, :, c0:c1].rearrange("p j (c i) -> p c j i", i=4)
            if on_scalar:
                nc.scalar.copy(out=dst, in_=src)
            else:
                nc.vector.tensor_copy(out=dst, in_=src)

        def quantize_w(i):
            pc = pieces[i]
            nc.vector.quantize_mx(
                out=w_codes[pc][:].bitcast(FP8X4),
                scales=w_scales[pc][:],
                in_=grouped[pc][:].rearrange("p n j -> p (n j)"),
            )

        acc, spare, summed, y_bf16, turned, y_grouped = {}, {}, {}, {}, {}, {}

        def multiply(u, order):
            h, t0, nt = units[u]
            for i, m in order:
                bank = acc_pool.tile([P, GROUP], F32, name="acc")
                acc[u, i, m] = bank
                if u in SUMMED_ON_TENSOR:
                    beams = slice((2 * i + m) * P, (2 * i + m + 1) * P)
                    tokens = slice(t0 * P, (t0 + 2) * P)
                    for part in range(2):
                        for g in range(KG):
                            nc.tensor.matmul_mx(
                                out=bank[:, part * 2 * P : (part + 1) * 2 * P],
                                lhsT=w_codes[h, part, g][:, beams].bitcast(FP8X4),
                                lhsT_scale=w_scales[h, part, g][:, beams],
                                rhs=xw[:, g, tokens].bitcast(FP8X4),
                                rhs_scale=xs[:, g, tokens],
                                start=(g == 0),
                                stop=(g == KG - 1),
                            )
                    continue
                tokens = slice((t0 + i) * P, (t0 + i + 1) * P)
                for g in range(KG):
                    nc.tensor.matmul_mx(
                        out=bank[:],
                        lhsT=xw[:, g, tokens].bitcast(FP8X4),
                        lhsT_scale=xs[:, g, tokens],
                        rhs=w_codes[h, m, g][:].bitcast(FP8X4),
                        rhs_scale=w_scales[h, m, g][:],
                        start=(g == 0),
                        stop=(g == KG - 1),
                    )

        def square(u, order):
            h, t0, nt = units[u]
            last = batch_of[u][-1]
            for i, m in order:
                if last not in spare:
                    if u in SUMMED_ON_TENSOR:
                        spare[last] = work.tile([P, 4, GROUP], F32, name="both", bufs=2)
                    else:
                        spare[last] = work.tile([P, 2, GROUP], F32, name="spare", bufs=5)
                if u in SUMMED_ON_TENSOR:
                    dst = spare[last][:, 2 * i + m, :]
                elif m == 0:
                    dst = y_f32[:, h, t0 + i, :]
                else:
                    dst = spare[last][:, t0 + i - batch_span(u)[1], :]
                nc.scalar.activation(out=dst, in_=acc[u, i, m][:], func=SQUARE)

        def add(u):
            h, t0, nt = batch_span(u)
            y = y_f32[:, h, t0 : t0 + nt, :]
            nc.vector.tensor_tensor(out=y, in0=y, in1=spare[u][:, :nt, :], op=ADD)

        def sum_on_tensor(u, tiles):
            for tt in tiles:
                summed[u, tt] = turn_pool.tile([P, GROUP], F32, name="turned")
                for bt in range(4):
                    for part in range(2):
                        c0 = part * 2 * P + tt * P
                        nc.tensor.matmul(
                            out=summed[u, tt][:, bt * P : (bt + 1) * P],
                            lhsT=spare[u][:, bt, c0 : c0 + P],
                            rhs=ident[:],
                            is_transpose=True,
                            start=(part == 0),
                            stop=(part == 1),
                        )

        def apply_gain(u, tiles):
            h, t0, nt = batch_span(u)
            y = y_f32[:, h, t0 : t0 + nt, :]
            if u in SUMMED_ON_TENSOR:
                for tt in tiles:
                    nc.vector.tensor_tensor(out=y[:, tt, :], in0=summed[u, tt][:], in1=gain_sb[:, h, :], op=MULT)
            else:
                row = gain_sb[:, h, :].unsqueeze(1).to_broadcast([P, nt, GROUP])
                nc.vector.tensor_tensor(out=y, in0=y, in1=row, op=MULT)

        def store_y(u):
            h, t0, nt = batch_span(u)
            y = y_f32[:, h, t0 : t0 + nt, :]
            dst = out_0[t0 * P : (t0 + nt) * P, h * GROUP : (h + 1) * GROUP]
            nc.sync.dma_start(out=dst.rearrange("(i p) b -> p i b", p=P), in_=y)

        def round_bf16(u, on_scalar):
            h, t0, nt = batch_span(u)
            y_bf16[u] = work.tile([P, 2 * GROUP], BF16, name="y_bf16")
            y = y_f32[:, h, t0 : t0 + nt, :]
            if nt == 1:
                dst = y_bf16[u][:, :GROUP].rearrange("p (w a m e) -> p a w m e", a=2, w=2, e=2)
                src = y.rearrange("p i (a m w e) -> p (i a) w m e", a=2, w=2, e=2)
            else:
                dst = y_bf16[u][:, : nt * GROUP].rearrange("p (i w m e) -> p i w m e", i=nt, w=2, e=2)
                src = y.rearrange("p i (m w e) -> p i w m e", w=2, e=2)
            if on_scalar:
                nc.scalar.copy(out=dst, in_=src)
            elif u in ROUND_ON_GPSIMD:
                nc.gpsimd.tensor_scalar(out=dst, in0=src, scalar1=1.0, scalar2=0.0, op0=MULT, op1=ADD)
            else:
                nc.vector.tensor_copy(out=dst, in_=src)

        def turn(u):
            h, t0, nt = units[u]
            words = y_bf16[batch_of[u][-1]][:].bitcast(F32)
            turned[u] = turn_pool.tile([P, 2, 2 * P], F32, name="turned")
            for i in range(nt):
                for w in range(2):
                    c0 = (2 * (t0 + i - batch_span(u)[1]) + w) * P
                    nc.tensor.transpose(turned[u][:, w, i * P : (i + 1) * P], words[:, c0 : c0 + P], ident[:])

        def leave_psum(u, on_scalar):
            h, t0, nt = units[u]
            last = batch_of[u][-1]
            if last not in y_grouped:
                y_grouped[last] = work.tile([P, 2 * GROUP], BF16, name="y_grouped", align_bytes=64)
            c0 = (t0 - batch_span(u)[1]) * GROUP
            dst = y_grouped[last][:, c0 : c0 + nt * GROUP].bitcast(F32).rearrange("p (n w) -> p n w", w=2)
            src = turned[u][:, :, : nt * P].rearrange("p w n -> p n w")
            if not on_scalar:
                nc.vector.tensor_copy(out=dst, in_=src)
            else:
                nc.scalar.copy(out=dst, in_=src)

        def quantize_y(u):
            h, t0, nt = batch_span(u)
            c0, c1 = t0 * P, (t0 + nt) * P
            nc.vector.quantize_mx(
                out=y_words[:, h, c0:c1].bitcast(FP8X4),
                scales=y_scales[:, h, c0:c1],
                in_=y_grouped[u][:, : nt * GROUP],
            )

        def store_words(u):
            h, t0, nt = batch_span(u)
            c1 = (t0 + nt) * P
            word_cuts = [0, 512, 1024, T] if h == 0 else [0, 512, 1024, T]
            if c1 in word_cuts:
                w0 = word_cuts[word_cuts.index(c1) - 1]
                dst = out_1[h].rearrange("p n j -> p (n j)")[:, PACK * w0 : PACK * c1]
                nc.sync.dma_start(out=dst.bitcast(I32), in_=y_words[:, h, w0:c1].bitcast(I32))

        def store_scales(u, q):
            h, t0, nt = batch_span(u)
            c1 = (t0 + nt) * P
            scale_cuts = [0, T] if h == 0 else [0, T]
            if c1 in scale_cuts:
                w0 = scale_cuts[scale_cuts.index(c1) - 1]
                queues = [nc.scalar, nc.scalar, nc.sync, nc.scalar] if u == n_units - 1 else [nc.sync] * 4
                if True:
                    queues[q].dma_start(
                        out=out_2[h, 4 * q : 4 * q + 4, w0:c1].bitcast(I32),
                        in_=y_scales[32 * q : 32 * q + 4, h, w0:c1].bitcast(I32),
                    )

        def tile_order(u):
            return [(i, m) for i in range(units[u][2]) for m in range(2)]

        load_gain()
        load_x_scales()
        nc.scalar.activation(out=warm[:, 1:2], in_=warm[:, 0:1], func=SQUARE)
        load_w(0, 0, 512)
        interleave(0, 0, 256, True)
        load_w(1, 0, 512)
        interleave(0, 256, 512, False)
        interleave(1, 0, 256, False)
        load_w(2, 0, 512)
        interleave(1, 256, 512, True)
        quantize_w(0)
        interleave(2, 0, 256, False)
        load_w(3, 0, 512)
        load_x(0, 256)
        load_w(4, 0, 512)
        interleave(2, 256, 512, True)
        quantize_w(1)
        spread_gain()
        interleave(3, 0, 256, False)
        multiply(0, [(0, 0)])
        multiply(0, [(1, 0)])
        quantize_w(2)
        interleave(3, 256, 512, True)
        quantize_w(3)
        load_w(5, 0, 512)
        multiply(0, [(0, 1)])
        load_x(256, 768)
        multiply(0, [(1, 1)])
        interleave(4, 0, 256, True)
        square(0, [(1, 0)])
        square(0, [(0, 0)])
        multiply(1, [(0, 0)])
        multiply(1, [(0, 1)])
        square(0, [(1, 1)])
        square(0, [(0, 1)])
        square(1, [(0, 1)])
        square(1, [(0, 0)])
        load_w(6, 0, 512)
        multiply(1, [(1, 0)])
        multiply(1, [(1, 1)])
        multiply(2, [(0, 0)])
        square(1, [(1, 1)])
        multiply(2, [(0, 1)])
        multiply(2, [(1, 0)])
        leave_gain()
        square(1, [(1, 0)])
        load_x(768, 1536)
        square(2, [(0, 1)])
        multiply(2, [(1, 1)])
        square(2, [(0, 0)])
        load_w(7, 0, 512)
        multiply(3, [(0, 0)])
        multiply(3, [(0, 1)])
        interleave(5, 0, 256, False)
        interleave(5, 256, 512, False)
        interleave(4, 256, 512, False)
        interleave(6, 256, 512, False)
        multiply(3, [(1, 0)])
        add(0)
        square(2, [(1, 1)])
        quantize_w(4)
        square(2, [(1, 0)])
        quantize_w(5)
        square(3, [(0, 1)])
        square(3, [(0, 0)])
        multiply(3, [(1, 1)])
        square(3, [(1, 1)])
        square(3, [(1, 0)])
        multiply(4, [(0, 0)])
        multiply(4, [(0, 1)])
        multiply(4, [(1, 0)])
        add(1)
        multiply(4, [(1, 1)])
        interleave(6, 0, 256, False)
        interleave(7, 256, 512, False)
        square(4, [(0, 1)])
        apply_gain(0, [0])
        store_y(0)
        apply_gain(1, [0])
        store_y(1)
        quantize_w(6)
        multiply(5, [(0, 0)])
        interleave(7, 0, 256, False)
        square(4, [(0, 0)])
        square(4, [(1, 1)])
        add(3)
        round_bf16(0, True)
        square(4, [(1, 0)])
        multiply(5, [(0, 1)])
        sum_on_tensor(2, [0])
        quantize_w(7)
        square(5, [(0, 1)])
        square(5, [(0, 0)])
        sum_on_tensor(2, [1])
        multiply(5, [(1, 0)])
        multiply(5, [(1, 1)])
        apply_gain(2, [0])
        multiply(6, [(0, 0)])
        multiply(6, [(0, 1)])
        multiply(6, [(1, 0)])
        square(5, [(1, 1)])
        apply_gain(2, [1])
        store_y(2)
        round_bf16(1, False)
        round_bf16(2, False)
        add(4)
        square(5, [(1, 0)])
        multiply(6, [(1, 1)])
        multiply(7, [(0, 0)])
        apply_gain(3, [0])
        store_y(3)
        apply_gain(4, [0])
        store_y(4)
        square(6, [(0, 1)])
        turn(0)
        square(6, [(0, 0)])
        turn(1)
        leave_psum(0, False)
        square(6, [(1, 1)])
        square(6, [(1, 0)])
        multiply(7, [(0, 1)])
        round_bf16(3, False)
        add(6)
        multiply(7, [(1, 0)])
        leave_psum(1, True)
        multiply(7, [(1, 1)])
        quantize_y(0)
        sum_on_tensor(5, [0])
        square(7, [(0, 1)])
        turn(2)
        square(7, [(0, 0)])
        sum_on_tensor(5, [1])
        square(7, [(1, 1)])
        apply_gain(5, [0])
        square(7, [(1, 0)])
        multiply(8, [(0, 0)])
        multiply(8, [(0, 1)])
        leave_psum(2, True)
        round_bf16(4, True)
        add(7)
        multiply(8, [(1, 0)])
        multiply(8, [(1, 1)])
        apply_gain(5, [1])
        store_y(5)
        multiply(9, [(0, 0)])
        square(8, [(0, 1)])
        square(8, [(0, 0)])
        apply_gain(6, [0])
        store_y(6)
        round_bf16(5, False)
        square(8, [(1, 1)])
        multiply(9, [(0, 1)])
        turn(3)
        turn(4)
        quantize_y(1)
        store_words(1)
        square(8, [(1, 0)])
        turn(5)
        square(9, [(0, 1)])
        leave_psum(3, True)
        leave_psum(4, True)
        multiply(9, [(1, 0)])
        square(9, [(0, 0)])
        multiply(9, [(1, 1)])
        apply_gain(7, [0])
        store_y(7)
        sum_on_tensor(8, [0])
        round_bf16(6, False)
        sum_on_tensor(8, [1])
        multiply(10, [(0, 0)])
        quantize_y(2)
        multiply(10, [(0, 1)])
        square(9, [(1, 1)])
        square(9, [(1, 0)])
        quantize_y(3)
        store_words(3)
        round_bf16(7, True)
        square(10, [(0, 1)])
        multiply(10, [(1, 0)])
        square(10, [(0, 0)])
        leave_psum(5, False)
        quantize_y(4)
        apply_gain(8, [0])
        multiply(10, [(1, 1)])
        multiply(11, [(0, 0)])
        quantize_y(5)
        store_words(5)
        store_scales(5, 0)
        store_scales(5, 1)
        store_scales(5, 2)
        store_scales(5, 3)
        square(10, [(1, 1)])
        square(10, [(1, 0)])
        add(9)
        apply_gain(8, [1])
        store_y(8)
        apply_gain(9, [0])
        store_y(9)
        multiply(11, [(0, 1)])
        square(11, [(0, 1)])
        round_bf16(8, False)
        multiply(12, [(0, 0)])
        round_bf16(9, False)
        multiply(12, [(0, 1)])
        square(11, [(0, 0)])
        turn(6)
        square(12, [(0, 1)])
        square(12, [(0, 0)])
        add(10)
        add(11)
        leave_psum(6, True)
        apply_gain(10, [0])
        store_y(10)
        turn(7)
        add(12)
        turn(8)
        leave_psum(7, True)
        apply_gain(11, [0])
        store_y(11)
        apply_gain(12, [0])
        store_y(12)
        round_bf16(10, True)
        round_bf16(11, False)
        leave_psum(8, True)
        quantize_y(6)
        turn(9)
        turn(10)
        round_bf16(12, False)
        quantize_y(7)
        store_words(7)
        quantize_y(8)
        leave_psum(9, True)
        leave_psum(10, True)
        turn(11)
        quantize_y(9)
        store_words(9)
        turn(12)
        leave_psum(11, True)
        quantize_y(10)
        leave_psum(12, True)
        quantize_y(11)
        quantize_y(12)
        store_words(12)
        store_scales(12, 0)
        store_scales(12, 1)
        store_scales(12, 2)
        store_scales(12, 3)
